import numpy as np, ml_dtypes
CORES = [50,52,122,124]
N = 4
TOK, K = 32, 2
ROUTE = [[[0,1],[2,3],[0,3],[1,2],[1,2],[2,3],[2,3],[1,3],[0,1],[0,1],[0,3],[2,3],[1,3],[1,3],[0,3],[0,1],[0,1],[0,2],[0,3],[1,3],[1,3],[0,3],[1,3],[0,2],[0,1],[0,3],[0,3],[0,2],[0,2],[0,2],[0,3],[2,3]],[[0,1],[2,3],[0,2],[0,3],[1,3],[0,2],[0,2],[2,3],[1,3],[0,1],[2,3],[2,3],[0,3],[1,3],[1,3],[0,3],[1,3],[0,1],[0,3],[1,3],[1,3],[0,2],[0,2],[0,2],[1,3],[0,3],[0,1],[0,1],[0,1],[1,3],[2,3],[1,3]],[[0,2],[1,3],[1,2],[2,3],[0,1],[0,2],[1,2],[1,2],[2,3],[1,3],[2,3],[0,1],[1,3],[0,3],[0,2],[1,2],[1,2],[0,2],[1,3],[1,3],[1,3],[0,1],[1,3],[2,3],[0,2],[1,3],[0,3],[0,3],[0,1],[1,3],[2,3],[1,2]],[[1,2],[0,2],[2,3],[1,3],[1,3],[2,3],[1,3],[0,3],[1,2],[0,3],[2,3],[0,2],[1,3],[0,2],[2,3],[1,2],[0,2],[1,2],[1,3],[1,3],[1,2],[1,3],[0,3],[1,2],[0,1],[0,2],[0,2],[0,1],[0,3],[0,3],[0,3],[0,2]]]
def setup_inputs(rng):
    rt = (0.75 * rng.standard_normal((128, 1), dtype=np.float32) + rng.standard_normal((128, N), dtype=np.float32) / 2).astype(ml_dtypes.bfloat16)
    rm = np.zeros((N, N, TOK), np.float32)
    for r in range(N):
        for t in range(TOK): rm[r, ROUTE[r][t], t] = 1.0
    return {"x": rng.standard_normal((N, 128, TOK), dtype=np.float32).astype(ml_dtypes.bfloat16), "rt": np.broadcast_to(rt, (N, 128, N)).copy(), "rm": rm.astype(ml_dtypes.bfloat16), "w": rng.standard_normal((N, 128, 128), dtype=np.float32).astype(ml_dtypes.bfloat16)}
def setup_inputs_big(rng):
    d = setup_inputs(rng)
    for k in ("x", "w"): d[k] = (d[k].astype(np.float32) * 1024.0).astype(d[k].dtype)
    return d
def setup_inputs_small(rng):
    d = setup_inputs(rng)
    for k in ("x", "w"): d[k] = (d[k].astype(np.float32) * (1 / 1024.0)).astype(d[k].dtype)
    return d
def setup_inputs_apart(rng):
    d = setup_inputs(rng)
    f = (10.0 ** rng.permutation(np.linspace(-1.5, 1.5, N))).astype(np.float32).reshape(N, 1, 1)
    for k in ("x",): d[k] = (d[k].astype(np.float32) * f).astype(d[k].dtype)
    return d
def setup_inputs_lure(rng):
    d = setup_inputs(rng); x = d["x"].astype(np.float32) * 1024; rt = d["rt"][0].astype(np.float32)
    for r in range(N):
        for t in range(TOK):
            u = int(rng.choice([e for e in range(N) if e not in ROUTE[r][t]]))
            x[r][:, t] += 2097152 * (rt[:, u] - rt[:, ROUTE[r][t][0]])
    d["x"] = x.astype(d["x"].dtype)
    return d
def reference(x, rt, rm, w):
    X, RT, W = x.astype(np.float64), rt.astype(np.float64), w.astype(np.float64)
    y = np.zeros((N, 128, TOK))
    for r in range(N):
        sc = RT[r].T @ X[r]
        for t in range(TOK):
            ex = ROUTE[r][t]; g = np.exp(sc[ex, t] - sc[ex, t].max()); g = g / g.sum()
            y[r][:, t] = sum(g[i] * (W[e].T @ X[r][:, t]) for i, e in enumerate(ex))
    return {"y": y.astype(ml_dtypes.bfloat16)}

@@ -1,0 +1,223 @@
+from concourse.bass import DstId, RemoteDMATransfer
+from concourse.mybir import AluOpType, ActivationFunctionType
+
+N = 4
+TOK = 32
+NQ = 4
+HOP_ENGINES = 4
+
+SCRATCH = {
+    "wd": ("dram", [128, 128], "bfloat16"),
+    "wl0": ("sbuf", [128, 128], "bfloat16"),
+    "wl1": ("sbuf", [128, 128], "bfloat16"),
+    "wl2": ("sbuf", [128, 128], "bfloat16"),
+    "wl3": ("sbuf", [128, 128], "bfloat16"),
+    "xs": ("sbuf", [128, TOK], "bfloat16"),
+    "rts": ("sbuf", [128, N], "bfloat16"),
+    "rms": ("sbuf", [128, TOK], "bfloat16"),
+    "rmf": ("sbuf", [128, 128], "bfloat16"),
+    "one_b": ("sbuf", [128, 128], "bfloat16"),
+    "one_f": ("sbuf", [128, 128], "float32"),
+    "two_f": ("sbuf", [128, 128], "float32"),
+    "bd2": ("sbuf", [128, 128], "float32"),
+    "cm": ("sbuf", [128, 128], "float32"),
+    "z": ("sbuf", [128, 128], "float32"),
+    "xm": ("sbuf", [128, 128], "bfloat16"),
+    "xg": ("sbuf", [128, 128], "bfloat16"),
+    "ys": ("sbuf", [128, 128], "bfloat16"),
+    "ps_s": ("psum", [128, 512], "float32"),
+    "ps_m": ("psum", [128, 512], "float32"),
+    "ps_d": ("psum", [128, 512], "float32"),
+    "ps_y": ("psum", [128, 512], "float32"),
+}
+SEMAPHORES = ["l_wd", "l_x", "l_rt", "l_w", "l_rm", "l_rmf", "m_two", "m_oneb", "m_onef", "m_y", "g_bd",
+              "v_c", "v_z", "v_xm", "v_xg", "v_y", "p_s", "p_m", "p_d", "p_y", "a_sig", "s_y",
+              "hop", "sent", "a0", "a1", "a2", "a3"]
+
+
+def _bits(mask):
+    return [b for b in range(mask.bit_length()) if (mask >> b) & 1]
+
+
+def _mk(bits):
+    m = 0
+    for b in bits:
+        m |= 1 << b
+    return m
+
+
+def _pow2(n):
+    p = 1
+    while p * 2 <= n:
+        p *= 2
+    return p
+
+
+def _plan(T, topo):
+    cores = list(T.cores)
+    n = len(cores)
+    route = T.tables["ROUTE"]
+    need = [[any(e in tok for tok in route[r]) for e in range(n)] for r in range(n)]
+    taken = set(cores)
+    plan = {}
+    for s, cs in enumerate(cores):
+        mine = [c for c in range(topo.CHIPS * topo.CORES_PER_CHIP) if topo.chip(c) == topo.chip(cs)]
+        idle = sorted([c for c in mine if c not in taken], key=lambda c: (topo.die(c) != topo.die(cs), c))
+        pool = [cs] + idle
+        near = [d for d in range(n) if d != s and need[d][s] and topo.chip(cores[d]) == topo.chip(cs)]
+        far = [d for d in range(n) if d != s and need[d][s] and topo.chip(cores[d]) != topo.chip(cs)]
+        carrier = {}
+        for d in far:
+            c = [c for c in pool if topo.may_write(c, cores[d])][0]
+            pool.remove(c)
+            taken.add(c)
+            carrier[d] = c
+        handed = [d for d in far if carrier[d] != cs]
+        own = [d for d in far if carrier[d] == cs]
+        other = [c for c in mine if c != cs][0]
+        on = _bits(topo.mask(cs, other))
+        out = _bits(topo.mask(cs, cores[far[0]])) if far else []
+        stay = [b for b in on if b not in out]
+        k = min(HOP_ENGINES, _pow2(len(stay) // max(1, len(handed))))
+        for i, d in enumerate(handed):
+            c = carrier[d]
+            plan[(s, d)] = (c, _mk(stay[i * k:(i + 1) * k]), topo.mask(c, cores[d]))
+        for i, d in enumerate(own):
+            k2 = _pow2(len(out) // len(own))
+            plan[(s, d)] = (cs, 0, _mk(out[i * k2:(i + 1) * k2]))
+        free = stay if own else [b for b in on if b not in stay]
+        for i, d in enumerate(near):
+            k3 = _pow2(len(free) // len(near))
+            plan[(s, d)] = (cs, 0, _mk(free[i * k3:(i + 1) * k3]))
+    return plan
+
+
+def _count(mask):
+    return len(_bits(mask))
+
+
+def rank_program(g, core, T, topo):
+    cores = list(T.cores)
+    S = T.sem
+    plan = _plan(T, topo)
+    rank = T.rank_of(core)
+
+    if rank is None:
+        jobs = [(s, d, v) for (s, d), v in sorted(plan.items()) if v[0] == core]
+        got = 0
+        left = 0
+        for s, d, (c, hop, mask) in jobs:
+            got += _count(hop)
+            g.wait_ge(S.hop, got)
+            rid, pid, _se = topo.addr(cores[d])
+            g.remote_dma(T["wl%d" % s][:, :], T.wd[:, :], S["a%d" % s], S.sent, pid, rid, mask)
+            left += _count(mask)
+        if jobs:
+            g.wait_ge(S.sent, left)
+        return
+
+    r = rank
+    v, pe, act, sy = g.vector, g.tensor, g.scalar, g.sync
+
+    def blk(e):
+        return slice(e * TOK, (e + 1) * TOK)
+
+    sy.dma_start(out=T.wd[:, :], in_=T.w[:, :]).then_inc(S.l_wd, 16)
+    sy.dma_start(out=T.xs[:, :], in_=T.x[:, :]).then_inc(S.l_x, 16)
+    sy.dma_start(out=T.rts[:, :], in_=T.rt[:, :]).then_inc(S.l_rt, 16)
+    sy.dma_start(out=T["wl%d" % r][:, :], in_=T.w[:, :]).then_inc(S.l_w, 16)
+    act.dma_start(out=T.rms[0:N, :], in_=T.rm[:, :]).then_inc(S.l_rm, 16)
+    act.dma_start(out=T.rmf[0:1, :], in_=T.rm[:, :]).then_inc(S.l_rmf, 16)
+
+    g.wait_ge(S.m_two, 1)
+    g.affine_select(out=T.bd2[0:N, :], in_=T.two_f[0:N, :], pattern=[[1, N], [0, TOK]],
+                    compare_op=AluOpType.is_equal, fill=0.0, base=0, channel_multiplier=-1).then_inc(S.g_bd, 1)
+    mine = [(d, plan[(r, d)]) for d in range(N) if (r, d) in plan]
+    handed = [(d, p) for d, p in mine if p[0] != core]
+    own = [(d, p) for d, p in mine if p[0] == core and topo.chip(cores[d]) != topo.chip(core)]
+    near = [(d, p) for d, p in mine if p[0] == core and topo.chip(cores[d]) == topo.chip(core)]
+    left = 0
+    g.wait_ge(S.l_wd, 16)
+    if handed:
+        trs = []
+        for d, (c, hop, mask) in handed:
+            rid, pid, _se = topo.addr(c)
+            trs.append(RemoteDMATransfer(dst_ids=[DstId(rid=rid, pnc=pid)], dma_engine_mask=hop, remote_sem=S.hop,
+                                         src=T.wd[:, :], dst=T.wd[:, :]))
+            left += _count(hop)
+        g.remote_dma_fused(trs, local_sem=S.sent)
+    for grp in (own, near):
+        if grp:
+            trs = []
+            for d, (c, hop, mask) in grp:
+                rid, pid, _se = topo.addr(cores[d])
+                trs.append(RemoteDMATransfer(dst_ids=[DstId(rid=rid, pnc=pid)], dma_engine_mask=mask,
+                                             remote_sem=S["a%d" % r], src=T.wd[:, :], dst=T["wl%d" % r][:, :]))
+                left += _count(mask)
+            g.remote_dma_fused(trs, local_sem=S.sent)
+    g.wait_ge(S.sent, left)
+
+    v.memset(T.two_f[0:N, :], 2.0).then_inc(S.m_two, 1)
+    v.memset(T.one_b[0:1, :], 1.0).then_inc(S.m_oneb, 1)
+    v.memset(T.one_f[0:N, :], 1.0).then_inc(S.m_onef, 1)
+    v.memset(T.ps_y[0:128 // NQ, 0:NQ * TOK], 0.0).then_inc(S.m_y, 1)
+    v.wait_ge(S.g_bd, 1)
+    v.wait_ge(S.l_rm, 16)
+    for e in range(N):
+        v.tensor_tensor(out=T.cm[0:N, blk(e)], in0=T.bd2[0:N, blk(e)], in1=T.rms[0:N, :],
+                        op=AluOpType.subtract).then_inc(S.v_c, 1)
+    v.wait_ge(S.v_c, N)
+    v.wait_ge(S.p_s, N)
+    v.tensor_tensor(out=T.z[0:N, :], in0=T.cm[0:N, :], in1=T.ps_s[0:N, 0:N * TOK],
+                    op=AluOpType.mult).then_inc(S.v_z, 1)
+    v.wait_ge(S.p_m, 1)
+    v.wait_ge(S.l_x, 16)
+    for e in range(N):
+        v.tensor_tensor(out=T.xm[:, blk(e)], in0=T.xs[:, :], in1=T.ps_m[:, blk(e)],
+                        op=AluOpType.mult).then_inc(S.v_xm, 1)
+    v.wait_ge(S.v_xm, N)
+    v.wait_ge(S.a_sig, 1)
+    v.tensor_tensor(out=T.xg[:, :], in0=T.xm[:, :], in1=T.ps_d[:, 0:N * TOK],
+                    op=AluOpType.mult).then_inc(S.v_xg, 1)
+
+    pe.wait_ge(S.l_x, 16)
+    pe.wait_ge(S.l_rt, 16)
+    for e in range(N):
+        pe.matmul(out=T.ps_s[0:N, blk(e)], lhsT=T.rts[:, :], rhs=T.xs[:, :], start=True, stop=True).then_inc(S.p_s, 1)
+    pe.wait_ge(S.m_oneb, 1)
+    pe.wait_ge(S.l_rmf, 16)
+    pe.matmul(out=T.ps_m[:, 0:N * TOK], lhsT=T.one_b[0:1, :], rhs=T.rmf[0:1, :], start=True, stop=True).then_inc(S.p_m, 1)
+    pe.wait_ge(S.m_onef, 1)
+    pe.wait_ge(S.v_z, 1)
+    pe.matmul(out=T.ps_d[:, 0:N * TOK], lhsT=T.one_f[0:N, :], rhs=T.z[0:N, :], start=True, stop=True).then_inc(S.p_d, 1)
+
+    act.wait_ge(S.p_d, 1)
+    act.activation(out=T.ps_d[:, 0:N * TOK], in_=T.ps_d[:, 0:N * TOK],
+                   func=ActivationFunctionType.Sigmoid).then_inc(S.a_sig, 1)
+
+    def late(e):
+        if e == r:
+            return 0
+        c = plan[(e, r)][0]
+        if topo.chip(cores[e]) == topo.chip(core):
+            return 1
+        return 2 if c == cores[e] else 3
+    order = sorted([e for e in range(N) if e == r or (e, r) in plan], key=lambda e: (late(e), e))
+    pe.wait_ge(S.v_xg, 1)
+    pe.wait_ge(S.m_y, 1)
+    n_mm = 0
+    for i, e in enumerate(order):
+        if e == r:
+            pe.wait_ge(S.l_w, 16)
+        else:
+            pe.wait_ge(S["a%d" % e], _count(plan[(e, r)][2]))
+        for q in range(NQ):
+            pe.matmul(out=T.ps_y[0:128 // NQ, q * TOK:(q + 1) * TOK], lhsT=T["wl%d" % e][:, q::NQ],
+                      rhs=T.xg[:, blk(e)], start=(n_mm == 0),
+                      stop=(n_mm == len(order) * NQ - 1)).then_inc(S.p_y, 1)
+            n_mm += 1
+    v.wait_ge(S.p_y, n_mm)
+    v.tensor_copy(out=T.ys[0:128 // NQ, :], in_=T.ps_y[0:128 // NQ, 0:NQ * TOK]).then_inc(S.v_y, 1)
+    sy.wait_ge(S.v_y, 1)
+    sy.dma_start(out=T.y[:, :], in_=T.ys[0:128 // NQ, :]).then_inc(S.s_y, 16)
+    sy.wait_ge(S.s_y, 16)

@@ -8,6 +8,7 @@ HOP_ENGINES = 4
 
 SCRATCH = {
     "wd": ("dram", [128, 128], "bfloat16"),
+    "wr": ("dram", [128, 128], "bfloat16"),
     "wl0": ("sbuf", [128, 128], "bfloat16"),
     "wl1": ("sbuf", [128, 128], "bfloat16"),
     "wl2": ("sbuf", [128, 128], "bfloat16"),
@@ -28,10 +29,11 @@ SCRATCH = {
     "ps_s": ("psum", [128, 512], "float32"),
     "ps_m": ("psum", [128, 512], "float32"),
     "ps_d": ("psum", [128, 512], "float32"),
-    "ps_y": ("psum", [128, 512], "float32"),
+    "ps_y0": ("psum", [128, 512], "float32"),
+    "ps_y1": ("psum", [128, 512], "float32"),
 }
 SEMAPHORES = ["l_wd", "l_x", "l_rt", "l_w", "l_rm", "l_rmf", "m_two", "m_oneb", "m_onef", "m_y", "g_bd",
-              "v_c", "v_z", "v_xm", "v_xg", "v_y", "p_s", "p_m", "p_d", "p_y", "a_sig", "s_y",
+              "v_c", "v_z", "v_xm", "v_xg", "v_y", "p_s", "p_m", "p_d", "p_y0", "p_y1", "a_sig", "s_y",
               "hop", "sent", "a0", "a1", "a2", "a3"]
 
 
@@ -53,47 +55,44 @@ def _pow2(n):
     return p
 
 
+def _count(mask):
+    return len(_bits(mask))
+
+
+def _split(bits, dsts):
+    k = _pow2(len(bits) // max(1, len(dsts)))
+    return {d: _mk(bits[i * k:(i + 1) * k]) for i, d in enumerate(dsts)}
+
+
 def _plan(T, topo):
     cores = list(T.cores)
     n = len(cores)
     route = T.tables["ROUTE"]
     need = [[any(e in tok for tok in route[r]) for e in range(n)] for r in range(n)]
-    taken = set(cores)
-    plan = {}
+    base = {}
     for s, cs in enumerate(cores):
         mine = [c for c in range(topo.CHIPS * topo.CORES_PER_CHIP) if topo.chip(c) == topo.chip(cs)]
-        idle = sorted([c for c in mine if c not in taken], key=lambda c: (topo.die(c) != topo.die(cs), c))
-        pool = [cs] + idle
         near = [d for d in range(n) if d != s and need[d][s] and topo.chip(cores[d]) == topo.chip(cs)]
         far = [d for d in range(n) if d != s and need[d][s] and topo.chip(cores[d]) != topo.chip(cs)]
-        carrier = {}
-        for d in far:
-            c = [c for c in pool if topo.may_write(c, cores[d])][0]
-            pool.remove(c)
-            taken.add(c)
-            carrier[d] = c
-        handed = [d for d in far if carrier[d] != cs]
-        own = [d for d in far if carrier[d] == cs]
-        other = [c for c in mine if c != cs][0]
-        on = _bits(topo.mask(cs, other))
-        out = _bits(topo.mask(cs, cores[far[0]])) if far else []
+        pool = [cs] + [c for c in cores if c != cs and c in mine] + [c for c in mine if c not in cores]
+        c = [c for c in pool if all(topo.may_write(c, cores[d]) for d in far)][0]
+        on = _bits(topo.mask(cs, [k for k in mine if k != cs][0]))
+        out = _bits(topo.mask(c, cores[far[0]])) if far else []
         stay = [b for b in on if b not in out]
-        k = min(HOP_ENGINES, _pow2(len(stay) // max(1, len(handed))))
-        for i, d in enumerate(handed):
-            c = carrier[d]
-            plan[(s, d)] = (c, _mk(stay[i * k:(i + 1) * k]), topo.mask(c, cores[d]))
-        for i, d in enumerate(own):
-            k2 = _pow2(len(out) // len(own))
-            plan[(s, d)] = (cs, 0, _mk(out[i * k2:(i + 1) * k2]))
-        free = stay if own else [b for b in on if b not in stay]
-        for i, d in enumerate(near):
-            k3 = _pow2(len(free) // len(near))
-            plan[(s, d)] = (cs, 0, _mk(free[i * k3:(i + 1) * k3]))
+        free = stay if c == cs else [b for b in on if b not in stay]
+        base[s] = (c, near, far, out, stay, free)
+    plan = {}
+    for s, cs in enumerate(cores):
+        c, near, far, out, stay, free = base[s]
+        hop = 0 if c == cs else _mk(stay[::max(1, len(stay) // HOP_ENGINES)][0:HOP_ENGINES])
+        fwd, wm = None, {}
+        fm = _split(out, far)
+        if c == cs and len(far) > 1:
+            fwd = sorted(far, key=lambda d: (base[d][0] == cores[d], d))[0]
+            fm = _split(out, [fwd])
+            wm = _split(base[fwd][5], [d for d in far if d != fwd])
+        plan[s] = (c, hop, fm, _split(free, near), fwd, wm)
     return plan
-
-
-def _count(mask):
-    return len(_bits(mask))
 
 
 def rank_program(g, core, T, topo):
@@ -101,23 +100,38 @@ def rank_program(g, core, T, topo):
     S = T.sem
     plan = _plan(T, topo)
     rank = T.rank_of(core)
+    left = [0]
+
+    def send(s, src, masks):
+        trs = []
+        for d, mask in sorted(masks.items()):
+            rid, pid, _se = topo.addr(cores[d])
+            trs.append(RemoteDMATransfer(dst_ids=[DstId(rid=rid, pnc=pid)], dma_engine_mask=mask,
+                                         remote_sem=S["a%d" % s], src=src, dst=T["wl%d" % s][:, :]))
+            left[0] += _count(mask)
+        if trs:
+            g.remote_dma_fused(trs, local_sem=S.sent)
+
+    def carry():
+        got = 0
+        for s in sorted(plan):
+            if plan[s][0] == core and cores[s] != core:
+                got += _count(plan[s][1])
+                g.wait_ge(S.hop, got)
+                send(s, T.wr[:, :], plan[s][2])
 
     if rank is None:
-        jobs = [(s, d, v) for (s, d), v in sorted(plan.items()) if v[0] == core]
-        got = 0
-        left = 0
-        for s, d, (c, hop, mask) in jobs:
-            got += _count(hop)
-            g.wait_ge(S.hop, got)
-            rid, pid, _se = topo.addr(cores[d])
-            g.remote_dma(T["wl%d" % s][:, :], T.wd[:, :], S["a%d" % s], S.sent, pid, rid, mask)
-            left += _count(mask)
-        if jobs:
-            g.wait_ge(S.sent, left)
+        carry()
+        if left[0]:
+            g.wait_ge(S.sent, left[0])
         return
 
     r = rank
     v, pe, act, sy = g.vector, g.tensor, g.scalar, g.sync
+    P = 128 // NQ
+    H = NQ // 2 * TOK
+    ps_y = [T.ps_y0, T.ps_y1]
+    p_y = [S.p_y0, S.p_y1]
 
     def blk(e):
         return slice(e * TOK, (e + 1) * TOK)
@@ -132,35 +146,27 @@ def rank_program(g, core, T, topo):
     g.wait_ge(S.m_two, 1)
     g.affine_select(out=T.bd2[0:N, :], in_=T.two_f[0:N, :], pattern=[[1, N], [0, TOK]],
                     compare_op=AluOpType.is_equal, fill=0.0, base=0, channel_multiplier=-1).then_inc(S.g_bd, 1)
-    mine = [(d, plan[(r, d)]) for d in range(N) if (r, d) in plan]
-    handed = [(d, p) for d, p in mine if p[0] != core]
-    own = [(d, p) for d, p in mine if p[0] == core and topo.chip(cores[d]) != topo.chip(core)]
-    near = [(d, p) for d, p in mine if p[0] == core and topo.chip(cores[d]) == topo.chip(core)]
-    left = 0
+    c, hop, fm, nm, fwd, wm = plan[r]
     g.wait_ge(S.l_wd, 16)
-    if handed:
-        trs = []
-        for d, (c, hop, mask) in handed:
-            rid, pid, _se = topo.addr(c)
-            trs.append(RemoteDMATransfer(dst_ids=[DstId(rid=rid, pnc=pid)], dma_engine_mask=hop, remote_sem=S.hop,
-                                         src=T.wd[:, :], dst=T.wd[:, :]))
-            left += _count(hop)
-        g.remote_dma_fused(trs, local_sem=S.sent)
-    for grp in (own, near):
-        if grp:
-            trs = []
-            for d, (c, hop, mask) in grp:
-                rid, pid, _se = topo.addr(cores[d])
-                trs.append(RemoteDMATransfer(dst_ids=[DstId(rid=rid, pnc=pid)], dma_engine_mask=mask,
-                                             remote_sem=S["a%d" % r], src=T.wd[:, :], dst=T["wl%d" % r][:, :]))
-                left += _count(mask)
-            g.remote_dma_fused(trs, local_sem=S.sent)
-    g.wait_ge(S.sent, left)
+    if c != core:
+        rid, pid, _se = topo.addr(c)
+        g.remote_dma(T.wr[:, :], T.wd[:, :], S.hop, S.sent, pid, rid, hop)
+        left[0] += _count(hop)
+    else:
+        send(r, T.wd[:, :], fm)
+    send(r, T.wd[:, :], nm)
+    carry()
+    for s in sorted(plan):
+        if plan[s][4] == r:
+            g.wait_ge(S["a%d" % s], _count(plan[s][2][r]))
+            send(s, T["wl%d" % s][:, :], plan[s][5])
+    g.wait_ge(S.sent, left[0])
 
     v.memset(T.two_f[0:N, :], 2.0).then_inc(S.m_two, 1)
     v.memset(T.one_b[0:1, :], 1.0).then_inc(S.m_oneb, 1)
     v.memset(T.one_f[0:N, :], 1.0).then_inc(S.m_onef, 1)
-    v.memset(T.ps_y[0:128 // NQ, 0:NQ * TOK], 0.0).then_inc(S.m_y, 1)
+    for b in range(2):
+        v.memset(ps_y[b][0:P, 0:H], 0.0).then_inc(S.m_y, 1)
     v.wait_ge(S.g_bd, 1)
     v.wait_ge(S.l_rm, 16)
     for e in range(N):
@@ -195,29 +201,32 @@ def rank_program(g, core, T, topo):
     act.activation(out=T.ps_d[:, 0:N * TOK], in_=T.ps_d[:, 0:N * TOK],
                    func=ActivationFunctionType.Sigmoid).then_inc(S.a_sig, 1)
 
-    def late(e):
+    def how(e):
         if e == r:
-            return 0
-        c = plan[(e, r)][0]
-        if topo.chip(cores[e]) == topo.chip(core):
-            return 1
-        return 2 if c == cores[e] else 3
-    order = sorted([e for e in range(N) if e == r or (e, r) in plan], key=lambda e: (late(e), e))
+            return 0, 0
+        if r in plan[e][3]:
+            return 1, plan[e][3][r]
+        if r in plan[e][5]:
+            return 3, plan[e][5][r]
+        if r in plan[e][2]:
+            return (2 if plan[e][0] == cores[e] else 4), plan[e][2][r]
+        return None
+    order = sorted([e for e in range(N) if how(e)], key=lambda e: (how(e)[0], e))
     pe.wait_ge(S.v_xg, 1)
-    pe.wait_ge(S.m_y, 1)
-    n_mm = 0
+    pe.wait_ge(S.m_y, 2)
     for i, e in enumerate(order):
         if e == r:
             pe.wait_ge(S.l_w, 16)
         else:
-            pe.wait_ge(S["a%d" % e], _count(plan[(e, r)][2]))
+            pe.wait_ge(S["a%d" % e], _count(how(e)[1]))
         for q in range(NQ):
-            pe.matmul(out=T.ps_y[0:128 // NQ, q * TOK:(q + 1) * TOK], lhsT=T["wl%d" % e][:, q::NQ],
-                      rhs=T.xg[:, blk(e)], start=(n_mm == 0),
-                      stop=(n_mm == len(order) * NQ - 1)).then_inc(S.p_y, 1)
-            n_mm += 1
-    v.wait_ge(S.p_y, n_mm)
-    v.tensor_copy(out=T.ys[0:128 // NQ, :], in_=T.ps_y[0:128 // NQ, 0:NQ * TOK]).then_inc(S.v_y, 1)
-    sy.wait_ge(S.v_y, 1)
-    sy.dma_start(out=T.y[:, :], in_=T.ys[0:128 // NQ, :]).then_inc(S.s_y, 16)
+            b, k = divmod(q, NQ // 2)
+            pe.matmul(out=ps_y[b][0:P, k * TOK:(k + 1) * TOK], lhsT=T["wl%d" % e][:, q::NQ],
+                      rhs=T.xg[:, blk(e)], start=(i == 0 and k == 0),
+                      stop=(i == len(order) - 1 and k == NQ // 2 - 1)).then_inc(p_y[b], 1)
+    for b in range(2):
+        v.wait_ge(p_y[b], len(order) * NQ // 2)
+        v.tensor_copy(out=T.ys[0:P, b * H:(b + 1) * H], in_=ps_y[b][0:P, 0:H]).then_inc(S.v_y, 1)
+    sy.wait_ge(S.v_y, 2)
+    sy.dma_start(out=T.y[:, :], in_=T.ys[0:P, :]).then_inc(S.s_y, 16)
     sy.wait_ge(S.s_y, 16)

from concourse.bass import DstId, RemoteDMATransfer
from concourse.mybir import AluOpType, ActivationFunctionType

N = 4
TOK = 32
NQ = 4
HOP_ENGINES = 4

SCRATCH = {
    "wd": ("dram", [128, 128], "bfloat16"),
    "wr": ("dram", [128, 128], "bfloat16"),
    "wl0": ("sbuf", [128, 128], "bfloat16"),
    "wl1": ("sbuf", [128, 128], "bfloat16"),
    "wl2": ("sbuf", [128, 128], "bfloat16"),
    "wl3": ("sbuf", [128, 128], "bfloat16"),
    "xs": ("sbuf", [128, TOK], "bfloat16"),
    "rts": ("sbuf", [128, N], "bfloat16"),
    "rms": ("sbuf", [128, TOK], "bfloat16"),
    "rmf": ("sbuf", [128, 128], "bfloat16"),
    "one_b": ("sbuf", [128, 128], "bfloat16"),
    "one_f": ("sbuf", [128, 128], "float32"),
    "two_f": ("sbuf", [128, 128], "float32"),
    "bd2": ("sbuf", [128, 128], "float32"),
    "cm": ("sbuf", [128, 128], "float32"),
    "z": ("sbuf", [128, 128], "float32"),
    "xm": ("sbuf", [128, 128], "bfloat16"),
    "xg": ("sbuf", [128, 128], "bfloat16"),
    "ys": ("sbuf", [128, 128], "bfloat16"),
    "ps_s": ("psum", [128, 512], "float32"),
    "ps_m": ("psum", [128, 512], "float32"),
    "ps_d": ("psum", [128, 512], "float32"),
    "ps_y0": ("psum", [128, 512], "float32"),
    "ps_y1": ("psum", [128, 512], "float32"),
}
SEMAPHORES = ["l_wd", "l_x", "l_rt", "l_w", "l_rm", "l_rmf", "m_two", "m_oneb", "m_onef", "m_y", "g_bd",
              "v_c", "v_z", "v_xm", "v_xg", "v_y", "p_s", "p_m", "p_d", "p_y0", "p_y1", "a_sig", "s_y",
              "hop", "sent", "a0", "a1", "a2", "a3"]


def _bits(mask):
    return [b for b in range(mask.bit_length()) if (mask >> b) & 1]


def _mk(bits):
    m = 0
    for b in bits:
        m |= 1 << b
    return m


def _pow2(n):
    p = 1
    while p * 2 <= n:
        p *= 2
    return p


def _count(mask):
    return len(_bits(mask))


def _split(bits, dsts):
    k = _pow2(len(bits) // max(1, len(dsts)))
    return {d: _mk(bits[i * k:(i + 1) * k]) for i, d in enumerate(dsts)}


def _plan(T, topo):
    cores = list(T.cores)
    n = len(cores)
    route = T.tables["ROUTE"]
    need = [[any(e in tok for tok in route[r]) for e in range(n)] for r in range(n)]
    base = {}
    for s, cs in enumerate(cores):
        mine = [c for c in range(topo.CHIPS * topo.CORES_PER_CHIP) if topo.chip(c) == topo.chip(cs)]
        near = [d for d in range(n) if d != s and need[d][s] and topo.chip(cores[d]) == topo.chip(cs)]
        far = [d for d in range(n) if d != s and need[d][s] and topo.chip(cores[d]) != topo.chip(cs)]
        pool = [cs] + [c for c in cores if c != cs and c in mine] + [c for c in mine if c not in cores]
        c = [c for c in pool if all(topo.may_write(c, cores[d]) for d in far)][0]
        on = _bits(topo.mask(cs, [k for k in mine if k != cs][0]))
        out = _bits(topo.mask(c, cores[far[0]])) if far else []
        stay = [b for b in on if b not in out]
        free = stay if c == cs else [b for b in on if b not in stay]
        base[s] = (c, near, far, out, stay, free)
    plan = {}
    for s, cs in enumerate(cores):
        c, near, far, out, stay, free = base[s]
        hop = 0 if c == cs else _mk(stay[::max(1, len(stay) // HOP_ENGINES)][0:HOP_ENGINES])
        fwd, wm = None, {}
        fm = _split(out, far)
        if c == cs and len(far) > 1:
            fwd = sorted(far, key=lambda d: (base[d][0] == cores[d], d))[0]
            fm = _split(out, [fwd])
            wm = _split(base[fwd][5], [d for d in far if d != fwd])
        plan[s] = (c, hop, fm, _split(free, near), fwd, wm)
    return plan


def rank_program(g, core, T, topo):
    cores = list(T.cores)
    S = T.sem
    plan = _plan(T, topo)
    rank = T.rank_of(core)
    left = [0]

    def send(s, src, masks):
        trs = []
        for d, mask in sorted(masks.items()):
            rid, pid, _se = topo.addr(cores[d])
            trs.append(RemoteDMATransfer(dst_ids=[DstId(rid=rid, pnc=pid)], dma_engine_mask=mask,
                                         remote_sem=S["a%d" % s], src=src, dst=T["wl%d" % s][:, :]))
            left[0] += _count(mask)
        if trs:
            g.remote_dma_fused(trs, local_sem=S.sent)

    def carry():
        got = 0
        for s in sorted(plan):
            if plan[s][0] == core and cores[s] != core:
                got += _count(plan[s][1])
                g.wait_ge(S.hop, got)
                send(s, T.wr[:, :], plan[s][2])

    if rank is None:
        carry()
        if left[0]:
            g.wait_ge(S.sent, left[0])
        return

    r = rank
    v, pe, act, sy = g.vector, g.tensor, g.scalar, g.sync
    P = 128 // NQ
    H = NQ // 2 * TOK
    ps_y = [T.ps_y0, T.ps_y1]
    p_y = [S.p_y0, S.p_y1]

    def blk(e):
        return slice(e * TOK, (e + 1) * TOK)

    sy.dma_start(out=T.wd[:, :], in_=T.w[:, :]).then_inc(S.l_wd, 16)
    sy.dma_start(out=T.xs[:, :], in_=T.x[:, :]).then_inc(S.l_x, 16)
    sy.dma_start(out=T.rts[:, :], in_=T.rt[:, :]).then_inc(S.l_rt, 16)
    sy.dma_start(out=T["wl%d" % r][:, :], in_=T.w[:, :]).then_inc(S.l_w, 16)
    act.dma_start(out=T.rms[0:N, :], in_=T.rm[:, :]).then_inc(S.l_rm, 16)
    act.dma_start(out=T.rmf[0:1, :], in_=T.rm[:, :]).then_inc(S.l_rmf, 16)

    g.wait_ge(S.m_two, 1)
    g.affine_select(out=T.bd2[0:N, :], in_=T.two_f[0:N, :], pattern=[[1, N], [0, TOK]],
                    compare_op=AluOpType.is_equal, fill=0.0, base=0, channel_multiplier=-1).then_inc(S.g_bd, 1)
    c, hop, fm, nm, fwd, wm = plan[r]
    g.wait_ge(S.l_wd, 16)
    if c != core:
        rid, pid, _se = topo.addr(c)
        g.remote_dma(T.wr[:, :], T.wd[:, :], S.hop, S.sent, pid, rid, hop)
        left[0] += _count(hop)
    else:
        send(r, T.wd[:, :], fm)
    send(r, T.wd[:, :], nm)
    carry()
    for s in sorted(plan):
        if plan[s][4] == r:
            g.wait_ge(S["a%d" % s], _count(plan[s][2][r]))
            send(s, T["wl%d" % s][:, :], plan[s][5])
    g.wait_ge(S.sent, left[0])

    v.memset(T.two_f[0:N, :], 2.0).then_inc(S.m_two, 1)
    v.memset(T.one_b[0:1, :], 1.0).then_inc(S.m_oneb, 1)
    v.memset(T.one_f[0:N, :], 1.0).then_inc(S.m_onef, 1)
    for b in range(2):
        v.memset(ps_y[b][0:P, 0:H], 0.0).then_inc(S.m_y, 1)
    v.wait_ge(S.g_bd, 1)
    v.wait_ge(S.l_rm, 16)
    for e in range(N):
        v.tensor_tensor(out=T.cm[0:N, blk(e)], in0=T.bd2[0:N, blk(e)], in1=T.rms[0:N, :],
                        op=AluOpType.subtract).then_inc(S.v_c, 1)
    v.wait_ge(S.v_c, N)
    v.wait_ge(S.p_s, N)
    v.tensor_tensor(out=T.z[0:N, :], in0=T.cm[0:N, :], in1=T.ps_s[0:N, 0:N * TOK],
                    op=AluOpType.mult).then_inc(S.v_z, 1)
    v.wait_ge(S.p_m, 1)
    v.wait_ge(S.l_x, 16)
    for e in range(N):
        v.tensor_tensor(out=T.xm[:, blk(e)], in0=T.xs[:, :], in1=T.ps_m[:, blk(e)],
                        op=AluOpType.mult).then_inc(S.v_xm, 1)
    v.wait_ge(S.v_xm, N)
    v.wait_ge(S.a_sig, 1)
    v.tensor_tensor(out=T.xg[:, :], in0=T.xm[:, :], in1=T.ps_d[:, 0:N * TOK],
                    op=AluOpType.mult).then_inc(S.v_xg, 1)

    pe.wait_ge(S.l_x, 16)
    pe.wait_ge(S.l_rt, 16)
    for e in range(N):
        pe.matmul(out=T.ps_s[0:N, blk(e)], lhsT=T.rts[:, :], rhs=T.xs[:, :], start=True, stop=True).then_inc(S.p_s, 1)
    pe.wait_ge(S.m_oneb, 1)
    pe.wait_ge(S.l_rmf, 16)
    pe.matmul(out=T.ps_m[:, 0:N * TOK], lhsT=T.one_b[0:1, :], rhs=T.rmf[0:1, :], start=True, stop=True).then_inc(S.p_m, 1)
    pe.wait_ge(S.m_onef, 1)
    pe.wait_ge(S.v_z, 1)
    pe.matmul(out=T.ps_d[:, 0:N * TOK], lhsT=T.one_f[0:N, :], rhs=T.z[0:N, :], start=True, stop=True).then_inc(S.p_d, 1)

    act.wait_ge(S.p_d, 1)
    act.activation(out=T.ps_d[:, 0:N * TOK], in_=T.ps_d[:, 0:N * TOK],
                   func=ActivationFunctionType.Sigmoid).then_inc(S.a_sig, 1)

    def how(e):
        if e == r:
            return 0, 0
        if r in plan[e][3]:
            return 1, plan[e][3][r]
        if r in plan[e][5]:
            return 3, plan[e][5][r]
        if r in plan[e][2]:
            return (2 if plan[e][0] == cores[e] else 4), plan[e][2][r]
        return None
    order = sorted([e for e in range(N) if how(e)], key=lambda e: (how(e)[0], e))
    pe.wait_ge(S.v_xg, 1)
    pe.wait_ge(S.m_y, 2)
    for i, e in enumerate(order):
        if e == r:
            pe.wait_ge(S.l_w, 16)
        else:
            pe.wait_ge(S["a%d" % e], _count(how(e)[1]))
        for q in range(NQ):
            b, k = divmod(q, NQ // 2)
            pe.matmul(out=ps_y[b][0:P, k * TOK:(k + 1) * TOK], lhsT=T["wl%d" % e][:, q::NQ],
                      rhs=T.xg[:, blk(e)], start=(i == 0 and k == 0),
                      stop=(i == len(order) - 1 and k == NQ // 2 - 1)).then_inc(p_y[b], 1)
    for b in range(2):
        v.wait_ge(p_y[b], len(order) * NQ // 2)
        v.tensor_copy(out=T.ys[0:P, b * H:(b + 1) * H], in_=ps_y[b][0:P, 0:H]).then_inc(S.v_y, 1)
    sy.wait_ge(S.v_y, 2)
    sy.dma_start(out=T.y[:, :], in_=T.ys[0:P, :]).then_inc(S.s_y, 16)
    sy.wait_ge(S.s_y, 16)
